import numpy as np
import ml_dtypes


def mxq(x, axis, fmt="e4m3"):
    dtype, down = {"e4m3": (ml_dtypes.float8_e4m3fn, 7), "e5m2": (ml_dtypes.float8_e5m2, 14)}[fmt]
    v = np.moveaxis(np.asarray(x, np.float32).astype(ml_dtypes.bfloat16).astype(np.float64), axis, -1)
    blocks = v.reshape(v.shape[:-1] + (-1, 32))
    amax = np.abs(blocks).max(-1, keepdims=True)
    byte = np.maximum(np.where(amax > 0, np.frexp(amax)[1] - 1 + 127, 0) - down, 1)
    scale = np.exp2(byte - 127.0)
    codes = (blocks / scale).astype(np.float32).astype(dtype).astype(np.float64)
    return np.moveaxis((codes * scale).reshape(v.shape), -1, axis)


WIDE = False


def mx_kscale(k):
    if not WIDE:
        return np.ones(k)
    levels = np.array([10, -10, 5, -5, 0])
    if k % 512:
        return np.exp2(np.random.permutation(np.resize(levels, k // 32))).repeat(32)
    a = np.empty((k // 512, 16))
    for p in range(k // 512):
        a[p, :8] = np.random.permutation(np.resize(levels, 8))
        for g in range(8):
            far = levels[np.abs(levels - a[p, g]) >= 10]
            a[p, g + 8] = far[np.random.randint(len(far))]
    return np.exp2(a.ravel()).repeat(32)


BF16 = ml_dtypes.bfloat16


def bf(x):
    return np.asarray(x, np.float32).astype(BF16)


def f64(x):
    return np.asarray(x).astype(np.float64)


E2M1 = np.array([0.0, 0.5, 1.0, 1.5, 2.0, 3.0, 4.0, 6.0, -0.0, -0.5, -1.0, -1.5, -2.0, -3.0, -4.0, -6.0])


def pack_weight(w, fmt):
    k, n = w.shape
    w = f64(bf(w)).reshape(k // 32, 32, n)
    amax = np.abs(w).max(1)
    if fmt == "e4m3":
        byte = np.frexp(amax)[1] - 1 + 127 - 7
    else:
        mant, ex = np.frexp(amax / 6.0)
        byte = np.where(mant > 0.5, ex, ex - 1) + 127
    byte = np.clip(np.where(amax > 0, byte, 1), 1, 254)
    scaled = (w * np.exp2(127.0 - byte)[:, None, :]).reshape(k, n).astype(np.float32)
    by_word = np.ascontiguousarray(scaled.reshape(k // 512, 128, 4, n).transpose(0, 1, 3, 2))
    if fmt == "e4m3":
        words = by_word.astype(ml_dtypes.float8_e4m3fn).view(np.uint8)
    else:
        c = by_word.astype(ml_dtypes.float4_e2m1fn).view(np.uint8) & 0xF
        words = c[..., 0::2] | (c[..., 1::2] << 4)
    return np.ascontiguousarray(words), np.ascontiguousarray(byte.astype(np.uint8).reshape(k // 512, 16, n))


def unpack_weight(words, scales, fmt):
    g, p, n, _ = words.shape
    if fmt == "e4m3":
        vals = np.ascontiguousarray(words).view(ml_dtypes.float8_e4m3fn).astype(np.float64)
    else:
        nib = np.empty((g, p, n, 4), np.uint8)
        nib[..., 0::2] = words & 0xF
        nib[..., 1::2] = words >> 4
        vals = E2M1[nib]
    vals = vals * np.repeat(np.exp2(scales.astype(np.float64) - 127.0), 8, axis=1)[..., None]
    return vals.transpose(0, 1, 3, 2).reshape(g * 512, n)
def pack4(w):
    words, scales = pack_weight(w, "e2m1")
    return words.reshape(words.shape[0], 128, -1), scales


def unpack4(words, scales):
    return unpack_weight(words.reshape(words.shape[0], 128, -1, 2), scales, "e2m1")


def planes(Y):
    n, m = Y.shape
    b = f64(bf(Y)).reshape(n // 32, 32, m)
    amax = np.abs(b).max(1)
    byte = np.clip(np.where(amax > 0, np.frexp(amax)[1] - 1 + 127 - 7, 1), 1, 254)
    codes = (b * np.exp2(127.0 - byte)[:, None, :]).reshape(n, m).astype(np.float32).astype(ml_dtypes.float8_e4m3fn).view(np.uint8)
    words = codes.reshape(n // 512, 128, 4, m).transpose(0, 1, 3, 2)
    return np.ascontiguousarray(words), np.ascontiguousarray(byte.astype(np.uint8).reshape(n // 512, 16, m))


BLOCK, MODES, DOF = 512, 1024, 3072

SIZE_A, SIZE_B, SIZE_C = 0.8, 0.4, 0.4


def setup_inputs():
    noise = np.random.standard_normal
    s = mx_kscale(MODES)
    coef = noise((MODES, BLOCK)) * s[:, None]
    va = SIZE_A * noise((MODES, DOF)) / np.sqrt(MODES) / s[:, None]
    vb = SIZE_B * noise((MODES, DOF)) / np.sqrt(MODES) / s[:, None]
    vc = SIZE_C * noise((MODES, DOF)) / np.sqrt(MODES) / s[:, None]
    coef_words, coef_scales = pack_weight(coef, "e4m3")
    va_words, va_scales = pack4(va)
    vb_words, vb_scales = pack_weight(vb, "e4m3")
    x = bf(noise((BLOCK, DOF)))
    mass = bf(np.exp(0.8 * noise(DOF)))
    return {"coef_words": coef_words, "coef_scales": coef_scales,
            "va_words": va_words, "va_scales": va_scales,
            "vb_words": vb_words, "vb_scales": vb_scales,
            "vc": bf(vc), "x": x, "mass": mass}


def reference(coef_words, coef_scales, va_words, va_scales, vb_words, vb_scales, vc, x, mass):
    C = unpack_weight(coef_words, coef_scales, "e4m3")
    VA = unpack4(va_words, va_scales)
    VB = unpack_weight(vb_words, vb_scales, "e4m3")
    VC = mxq(f64(vc), 0, "e4m3")
    ea = C.T @ VA
    eb = C.T @ VB
    ec = C.T @ VC
    y = f64(mass) * (f64(x) - ea - eb - ec)
    words, scales = planes(y.T)
    return y, words, scales

@@ -1,0 +1,391 @@
+from contextlib import ExitStack
+
+import concourse.mybir as mybir
+from concourse.masks import make_identity
+
+BLOCK, MODES, DOF = 512, 1024, 3072
+FLOPS = 3 * 2 * BLOCK * MODES * DOF
+
+F32 = mybir.dt.float32
+BF16 = mybir.dt.bfloat16
+I32 = mybir.dt.int32
+U32 = mybir.dt.uint32
+U8 = mybir.dt.uint8
+FP8X4 = mybir.dt.float8_e4m3fn_x4
+FP4X4 = mybir.dt.float4_e2m1fn_x4
+SUB = mybir.AluOpType.subtract
+MUL = mybir.AluOpType.mult
+
+P = 128
+PACK = 4
+K_PASS = P * PACK
+GROUPS = MODES // K_PASS
+CHUNK = 512
+CHUNKS = DOF // CHUNK
+ROW_TILES = BLOCK // P
+TILES = CHUNKS * ROW_TILES
+HALF = CHUNK // 2
+QUADS = 4
+VB_ROW = 4
+MASS_RUN = DOF // P
+MASS_WORDS = MASS_RUN // 2
+ALIGN = 256
+SPANS = [(0, 1), (1, 2), (2, 3), (3, 4), (4, 6)]
+
+
+def tile_mass_weighted_basis_subtraction_k3_kernel(
+    tc, coef_words, coef_scales, va_words, va_scales, vb_words, vb_scales, vc, x, mass, out_0, out_1, out_2
+):
+    nc = tc.nc
+    with ExitStack() as ctx:
+        keep = ctx.enter_context(tc.tile_pool(name="keep", bufs=1))
+        work = ctx.enter_context(tc.tile_pool(name="work", bufs=1))
+        psum = ctx.enter_context(tc.psum_pool(name="psum", bufs=1))
+        ctx.enter_context(tc.manual_schedule())
+
+        def kept(name, shape, dtype):
+            return keep.tile(shape, dtype, name=name, align_bytes=ALIGN)
+
+        def rotating(tag, bufs, shape, dtype):
+            return work.tile(shape, dtype, name=tag, tag=tag, bufs=bufs, align_bytes=ALIGN)
+
+        def acc_bank(shape):
+            return psum.tile(shape, F32, name="acc", tag="acc", bufs=6)
+
+        def turn_bank():
+            return psum.tile([P, 4, P], F32, name="turn", tag="turn", bufs=2)
+
+        ident = kept("ident", [P, P], F32)
+        mass_run = kept("mass_run", [P, MASS_RUN], BF16)
+        mass_all = kept("mass_all", [P, DOF], BF16)
+        c_codes = [kept(f"c_codes{g}", [P, BLOCK], U32) for g in range(GROUPS)]
+        c_plane = kept("c_plane", [P, GROUPS, BLOCK], U8)
+        va_plane = kept("va_plane", [P, GROUPS, DOF], U8)
+        vb_plane = kept("vb_plane", [P, GROUPS, DOF], U8)
+        y_plane = kept("y_plane", [P, CHUNKS, BLOCK], U8)
+        y_codes = kept("y_codes", [P, CHUNKS, BLOCK], U32)
+        va_codes, vb_codes, vc_raw, x_sb, first_vc = {}, {}, {}, {}, {}
+
+        vc_grouped, vc_codes, vc_plane = {}, {}, {}
+        acc, y_sb, y_bf, turned, y_grouped = {}, {}, {}, {}, {}
+
+        def cols(j):
+            return slice(j * CHUNK, (j + 1) * CHUNK)
+
+        def load_scales(queue, plane, scales, row):
+            for r in range(4):
+                queue.dma_start(
+                    out=plane[row + r : P : 32].bitcast(I32),
+                    in_=scales[:, r:16:4, :].rearrange("g q n -> q g n").bitcast(I32),
+                )
+
+        def load_c(g):
+            nc.sync.dma_start(
+                out=c_codes[g][:].bitcast(I32), in_=coef_words[g].rearrange("p n t -> p (n t)").bitcast(I32)
+            )
+
+        def span_tile(name, span, lead, per_column, dtype, by_chunk):
+            first, end = span
+            tile = kept(f"{name}{first}", [P, lead, (end - first) * CHUNK * per_column], dtype)
+            for j in range(first, end):
+                by_chunk[j] = tile[:, :, (j - first) * CHUNK * per_column : (j - first + 1) * CHUNK * per_column]
+            return tile, slice(first * CHUNK, end * CHUNK)
+
+        def load_vc(span, g):
+            tile, n = span_tile(f"vc_raw{g}_", span, PACK, 1, BF16, vc_raw.setdefault(g, {}))
+            rows = vc[g * K_PASS : (g + 1) * K_PASS, n]
+            nc.sync.dma_start(out=tile[:], in_=rows.rearrange("(p t) n -> p t n", t=PACK))
+
+        def load_first_vc(h):
+            first_vc[h] = kept(f"first_vc{h}", [P, PACK, HALF], BF16)
+            rows = vc[:K_PASS, h * HALF : (h + 1) * HALF]
+            nc.sync.dma_start(out=first_vc[h][:], in_=rows.rearrange("(p t) n -> p t n", t=PACK))
+
+        def load_va(span):
+            tile, n = span_tile("va_codes", span, GROUPS, 2, U8, va_codes)
+            src = va_words.rearrange("g p b -> p g b")[:, :, 2 * n.start : 2 * n.stop]
+            nc.sync.dma_start(out=tile[:].bitcast(I32), in_=src.bitcast(I32))
+
+        def load_vb(span):
+            tile, n = span_tile("vb_codes", span, GROUPS, 1, U32, vb_codes)
+            src = vb_words.rearrange("g p n t -> p g (n t)")[:, :, 4 * n.start : 4 * n.stop]
+            nc.sync.dma_start(out=tile[:].bitcast(I32), in_=src.bitcast(I32))
+
+        def load_x(span):
+            tile, n = span_tile("x", span, ROW_TILES, 1, BF16, x_sb)
+            nc.sync.dma_start(out=tile[:], in_=x.rearrange("(r p) n -> p r n", p=P)[:, :, n])
+
+        def interleave(engine, j, g, n0, n1):
+            if n0 == 0:
+                vc_grouped[j, g] = rotating("vc_grouped", 3, [P, CHUNK * PACK], BF16)
+            dst = vc_grouped[j, g][:, n0 * PACK : n1 * PACK]
+            if (j, g) == (0, 0):
+                h = n0 // HALF
+                src = first_vc[h][:, :, n0 - h * HALF : n1 - h * HALF]
+            else:
+                src = vc_raw[g][j][:, :, n0:n1]
+            copy(engine, dst.rearrange("p (c i t) -> p c t i", i=4, t=PACK), src.rearrange("p t (c i) -> p c t i", i=4))
+
+        def copy(engine, out, in_):
+            if engine == "vector":
+                nc.vector.tensor_copy(out=out, in_=in_)
+            else:
+                nc.scalar.copy(out=out, in_=in_)
+
+        def quantize_vc(j, g):
+            vc_codes[j, g] = rotating("vc_codes", 4, [P, CHUNK], U32)
+            vc_plane[j, g] = rotating("vc_plane", 4, [P, CHUNK], U8)
+            nc.vector.quantize_mx(
+                out=vc_codes[j, g][:].bitcast(FP8X4), scales=vc_plane[j, g][:], in_=vc_grouped[j, g][:]
+            )
+
+        def mx_pass(i, part, g, start, stop):
+            j, r = divmod(i, ROW_TILES)
+            rows = slice(r * P, (r + 1) * P)
+            if start:
+                acc[i] = acc_bank([P, CHUNK])
+            if part == "a":
+                rhs, rhs_scale = va_codes[j][:, g, :].bitcast(FP4X4), va_plane[:, g, cols(j)]
+            elif part == "b":
+                rhs, rhs_scale = vb_codes[j][:, g, :].bitcast(FP8X4), vb_plane[VB_ROW:, g, cols(j)]
+            else:
+                rhs, rhs_scale = vc_codes[j, g][:].bitcast(FP8X4), vc_plane[j, g][:]
+            nc.tensor.matmul_mx(
+                out=acc[i][:],
+                lhsT=c_codes[g][:, rows].bitcast(FP8X4),
+                lhsT_scale=c_plane[:, g, rows],
+                rhs=rhs,
+                rhs_scale=rhs_scale,
+                start=start,
+                stop=stop,
+            )
+
+        def multiply(i, passes, opens, closes):
+            for n, (part, g) in enumerate(passes):
+                mx_pass(i, part, g, opens and n == 0, closes and n == len(passes) - 1)
+
+        def subtract(i):
+            j, r = divmod(i, ROW_TILES)
+            if r == 0:
+                y_sb[j] = rotating("y", 5, [P, ROW_TILES, CHUNK], F32)
+            nc.vector.tensor_tensor(out=y_sb[j][:, r, :], in0=x_sb[j][:, r, :], in1=acc[i][:], op=SUB)
+
+        def weigh(i):
+            j, r = divmod(i, ROW_TILES)
+            nc.vector.tensor_tensor(out=y_sb[j][:, r, :], in0=y_sb[j][:, r, :], in1=mass_all[:, cols(j)], op=MUL)
+
+        def in_word_order(ap):
+            return ap.rearrange("p (q u e) -> p u q e", u=2, e=2)
+
+        def round_y(engine, i):
+            j, r = divmod(i, ROW_TILES)
+            y_bf[i] = rotating("y_bf", 8, [P, CHUNK], BF16)
+            copy(engine, y_bf[i][:].rearrange("p (u q e) -> p u q e", u=2, e=2), in_word_order(y_sb[j][:, r, :]))
+
+        def weigh_and_round(i):
+            j, r = divmod(i, ROW_TILES)
+            y_bf[i] = rotating("y_bf", 8, [P, CHUNK], BF16)
+            nc.vector.tensor_tensor(
+                out=y_bf[i][:].rearrange("p (u q e) -> p u q e", u=2, e=2),
+                in0=in_word_order(y_sb[j][:, r, :]),
+                in1=in_word_order(mass_all[:, cols(j)]),
+                op=MUL,
+            )
+
+        def turn(first, count, bank):
+            turned[first] = bank
+            for n in range(count):
+                words = y_bf[first + n][:].bitcast(F32)
+                for u in range(2):
+                    nc.tensor.transpose(turned[first][:, 2 * n + u, :], words[:, u * P : (u + 1) * P], ident[:])
+
+        def unload(first, count):
+            j, r = divmod(first, ROW_TILES)
+            if r == 0:
+                y_grouped[j] = rotating("y_grouped", 2, [P, BLOCK * PACK], BF16)
+            dst = y_grouped[j][:].bitcast(F32)[:, 2 * r * P : 2 * (r + count) * P]
+            nc.scalar.copy(
+                out=dst.rearrange("p (n m u) -> p n m u", n=count, u=2),
+                in_=turned[first][:, : 2 * count, :].rearrange("p (n u) m -> p n m u", u=2),
+            )
+
+        def quantize_y(first, count):
+            j, r = divmod(first, ROW_TILES)
+            m = slice(r * P, (r + count) * P)
+            nc.vector.quantize_mx(
+                out=y_codes[:, j, m].bitcast(FP8X4),
+                scales=y_plane[:, j, m],
+                in_=y_grouped[j][:, PACK * r * P : PACK * (r + count) * P],
+            )
+
+        def store_y(first, count):
+            j, r = divmod(first, ROW_TILES)
+            dst = out_0.rearrange("(r p) n -> p r n", p=P)[:, r : r + count, cols(j)]
+            nc.sync.dma_start(out=dst, in_=y_sb[j][:, r : r + count, :])
+
+        def store_codes(queue, j0, j1, m0, m1):
+            dst = out_1.rearrange("g p m t -> p g (m t)").bitcast(I32)
+            queue.dma_start(out=dst[:, j0:j1, m0:m1], in_=y_codes[:, j0:j1, m0:m1].bitcast(I32))
+
+        def store_scales(j0, j1, queues):
+            for r in range(4):
+                queues[r % len(queues)].dma_start(
+                    out=out_2[j0:j1, r:16:4, :].rearrange("g q m -> q g m").bitcast(I32),
+                    in_=y_plane[r:P:32, j0:j1, :].bitcast(I32),
+                )
+
+        make_identity(nc, ident[:])
+        for plane in (c_plane, va_plane, vb_plane):
+            nc.vector.memset(plane[:].bitcast(I32), 0)
+        load_scales(nc.gpsimd, va_plane, va_scales, 0)
+        load_scales(nc.gpsimd, vb_plane, vb_scales, VB_ROW)
+        nc.sync.dma_start(out=mass_run[:], in_=mass.rearrange("(p w) -> p w", w=MASS_RUN))
+        load_first_vc(0)
+        load_first_vc(1)
+        load_c(0)
+        load_scales(nc.sync, c_plane, coef_scales, 0)
+        load_c(1)
+        load_va((0, 2))
+        load_vc(SPANS[0], 1)
+        load_vb(SPANS[0])
+        load_vc(SPANS[1], 0)
+        load_x(SPANS[0])
+        load_vc(SPANS[1], 1)
+        load_vb(SPANS[1])
+        load_x(SPANS[1])
+        for span in SPANS[2:]:
+            load_vc(span, 0)
+            load_vc(span, 1)
+            load_va(span)
+            load_vb(span)
+            load_x(span)
+
+        mass_words = mass_run[:].bitcast(F32)
+        mass_banks = [turn_bank(), turn_bank(), acc_bank([P, 4, P])]
+        for w in range(MASS_WORDS):
+            nc.tensor.transpose(mass_banks[w // 4][:, w % 4, :], mass_words[:, w : w + 1].to_broadcast([P, P]), ident[:])
+
+        interleave("vector", 0, 0, 0, HALF)
+        interleave("vector", 0, 0, HALF, 384)
+        interleave("scalar", 0, 0, 384, CHUNK)
+        quantize_vc(0, 0)
+        for b, bank in enumerate(mass_banks):
+            dst = mass_all[:].bitcast(F32).rearrange("p (n w) -> p n w", w=MASS_WORDS)[:, :, 4 * b : 4 * b + 4]
+            nc.scalar.copy(out=dst, in_=bank[:].rearrange("p w n -> p n w"))
+        interleave("vector", 0, 1, 0, 352)
+        interleave("scalar", 0, 1, 352, CHUNK)
+        quantize_vc(0, 1)
+        for r in range(ROW_TILES):
+            multiply(r, [("c", 0)], True, False)
+        for r in range(ROW_TILES):
+            multiply(r, [("a", 0), ("a", 1)], False, False)
+        for r in range(ROW_TILES):
+            multiply(r, [("c", 1)], False, False)
+        interleave("vector", 1, 0, 0, CHUNK)
+        quantize_vc(1, 0)
+        for s in range(TILES):
+            j, r = divmod(s, ROW_TILES)
+            if j == 0:
+                multiply(s, [("b", 0), ("b", 1)], False, True)
+            elif j == 1:
+                if r == 0:
+                    for i in range(s, s + ROW_TILES):
+                        multiply(i, [("a", 0), ("a", 1), ("c", 0)], True, False)
+                multiply(s, [("b", 0), ("b", 1), ("c", 1)], False, True)
+            else:
+                multiply(s, [("a", 0), ("a", 1), ("b", 0), ("b", 1), ("c", 0), ("c", 1)], True, True)
+            ahead = 1 <= j < CHUNKS - 1
+            final = j == CHUNKS - 1
+            if r == 0 and j >= 1:
+                subtract(s - 1)
+                if j > 1:
+                    round_y("vector", s - 2)
+                weigh(s - 1)
+                if final:
+                    store_y(s - 2, 2)
+                    unload(s - 8, 2)
+                    unload(s - 6, 2)
+                    round_y("scalar", s - 1)
+                else:
+                    store_y(s - 4, 4)
+                if ahead:
+                    interleave("scalar", j + 1, 0, 0, HALF)
+                    interleave("scalar", j + 1, 0, HALF, CHUNK)
+            elif r == 1:
+                if j == 0:
+                    interleave("scalar", 1, 1, 0, HALF)
+                    interleave("scalar", 1, 1, HALF, CHUNK)
+                subtract(s - 1)
+                if final:
+                    quantize_y(s - 9, ROW_TILES)
+                    store_codes(nc.sync, j - 3, j - 1, 0, BLOCK)
+                    store_scales(0, j - 1, [nc.sync])
+                weigh(s - 1)
+                if ahead:
+                    quantize_vc(j + 1, 0)
+                if final:
+                    store_y(s - 1, 1)
+                    turn(s - 5, 2, turn_bank())
+                    turn(s - 3, 2, turn_bank())
+                if ahead:
+                    interleave("scalar", j + 1, 1, 0, HALF)
+                    if j >= 2:
+                        unload(s - 9, 2)
+                    else:
+                        round_y("scalar", s - 3)
+            elif r == 2:
+                subtract(s - 1)
+                if ahead:
+                    round_y("vector", s - 3)
+                if final:
+                    round_y("vector", s - 2)
+                weigh(s - 1)
+                if ahead:
+                    interleave("scalar", j + 1, 1, HALF, CHUNK)
+                    if j >= 2:
+                        unload(s - 8, 2)
+                if final:
+                    unload(s - 6, 2)
+                    unload(s - 4, 2)
+                    round_y("scalar", s - 1)
+                    store_y(s - 1, 1)
+                if j == CHUNKS - 2:
+                    store_y(s - 2, 2)
+            elif r == 3:
+                if final:
+                    quantize_y(s - 7, 4)
+                    store_codes(nc.sync, j - 1, j, 0, BLOCK)
+                subtract(s - 1)
+                if not final:
+                    quantize_vc(j + 1, 1)
+                weigh(s - 1)
+                if ahead and j >= 2:
+                    quantize_y(s - 11, ROW_TILES)
+                    if j % 2 == 1:
+                        store_codes(nc.sync, j - 3, j - 1, 0, BLOCK)
+                if not final:
+                    round_y("scalar", s - 3)
+                    round_y("scalar", s - 2)
+                if ahead:
+                    turn(s - 7, 2, turn_bank())
+                    turn(s - 5, 2, turn_bank())
+
+        last = TILES - 1
+        store_y(last - 1, 1)
+        round_y("scalar", last - 1)
+        turn(last - 3, 2, acc_bank([P, 4, P]))
+        subtract(last)
+        unload(last - 3, 2)
+        weigh_and_round(last)
+        turn(last - 1, 1, acc_bank([P, 4, P]))
+        unload(last - 1, 1)
+        quantize_y(last - 3, 2)
+        weigh(last)
+        store_y(last, 1)
+        turn(last, 1, acc_bank([P, 4, P]))
+        quantize_y(last - 1, 1)
+        unload(last, 1)
+        store_codes(nc.sync, CHUNKS - 1, CHUNKS, 0, 3 * P)
+        quantize_y(last, 1)
+        store_codes(nc.scalar, CHUNKS - 1, CHUNKS, 3 * P, BLOCK)
+        store_scales(CHUNKS - 2, CHUNKS, [nc.sync, nc.scalar])

@@ -30,7 +30,10 @@ VB_ROW = 4
 MASS_RUN = DOF // P
 MASS_WORDS = MASS_RUN // 2
 ALIGN = 256
-SPANS = [(0, 1), (1, 2), (2, 3), (3, 4), (4, 6)]
+PASSES = 3 * GROUPS
+A, B, C0, C1 = [("a", 0), ("a", 1)], [("b", 0), ("b", 1)], [("c", 0)], [("c", 1)]
+VA_SPLIT = [0, 2 * CHUNK, DOF]
+VB_SPLIT = [0, 3 * CHUNK, DOF]
 
 
 def tile_mass_weighted_basis_subtraction_k3_kernel(
@@ -60,17 +63,21 @@ def tile_mass_weighted_basis_subtraction_k3_kernel(
         mass_all = kept("mass_all", [P, DOF], BF16)
         c_codes = [kept(f"c_codes{g}", [P, BLOCK], U32) for g in range(GROUPS)]
         c_plane = kept("c_plane", [P, GROUPS, BLOCK], U8)
-        va_plane = kept("va_plane", [P, GROUPS, DOF], U8)
-        vb_plane = kept("vb_plane", [P, GROUPS, DOF], U8)
+        va_plane = [kept(f"va_plane{h}", [P, GROUPS, VA_SPLIT[h + 1] - VA_SPLIT[h]], U8) for h in range(2)]
+        vb_plane = [kept(f"vb_plane{h}", [P, GROUPS, VB_SPLIT[h + 1] - VB_SPLIT[h]], U8) for h in range(2)]
         y_plane = kept("y_plane", [P, CHUNKS, BLOCK], U8)
         y_codes = kept("y_codes", [P, CHUNKS, BLOCK], U32)
         va_codes, vb_codes, vc_raw, x_sb, first_vc = {}, {}, {}, {}, {}
 
         vc_grouped, vc_codes, vc_plane = {}, {}, {}
-        acc, y_sb, y_bf, turned, y_grouped = {}, {}, {}, {}, {}
+        acc, passes_done, y_sb, y_bf, turned, y_grouped = {}, {}, {}, {}, {}, {}
 
         def cols(j):
             return slice(j * CHUNK, (j + 1) * CHUNK)
+
+        def plane_cols(planes, split, row, g, n):
+            h = 0 if n.start < split[1] else 1
+            return planes[h][row:, g, n.start - split[h] : n.stop - split[h]]
 
         def load_scales(queue, plane, scales, row):
             for r in range(4):
@@ -139,36 +146,39 @@ def tile_mass_weighted_basis_subtraction_k3_kernel(
                 out=vc_codes[j, g][:].bitcast(FP8X4), scales=vc_plane[j, g][:], in_=vc_grouped[j, g][:]
             )
 
-        def mx_pass(i, part, g, start, stop):
+        def multiply(i, passes, n0=0, n1=CHUNK):
             j, r = divmod(i, ROW_TILES)
             rows = slice(r * P, (r + 1) * P)
-            if start:
-                acc[i] = acc_bank([P, CHUNK])
-            if part == "a":
-                rhs, rhs_scale = va_codes[j][:, g, :].bitcast(FP4X4), va_plane[:, g, cols(j)]
-            elif part == "b":
-                rhs, rhs_scale = vb_codes[j][:, g, :].bitcast(FP8X4), vb_plane[VB_ROW:, g, cols(j)]
-            else:
-                rhs, rhs_scale = vc_codes[j, g][:].bitcast(FP8X4), vc_plane[j, g][:]
-            nc.tensor.matmul_mx(
-                out=acc[i][:],
-                lhsT=c_codes[g][:, rows].bitcast(FP8X4),
-                lhsT_scale=c_plane[:, g, rows],
-                rhs=rhs,
-                rhs_scale=rhs_scale,
-                start=start,
-                stop=stop,
-            )
+            n = slice(j * CHUNK + n0, j * CHUNK + n1)
+            for part, g in passes:
+                done = passes_done.get((i, n0), 0)
+                if done == 0:
+                    acc[i, n0] = acc_bank([P, n1 - n0])
+                if part == "a":
+                    rhs = va_codes[j][:, g, 2 * n0 : 2 * n1].bitcast(FP4X4)
+                    rhs_scale = plane_cols(va_plane, VA_SPLIT, 0, g, n)
+                elif part == "b":
+                    rhs = vb_codes[j][:, g, n0:n1].bitcast(FP8X4)
+                    rhs_scale = plane_cols(vb_plane, VB_SPLIT, VB_ROW, g, n)
+                else:
+                    rhs = vc_codes[j, g][:, n0:n1].bitcast(FP8X4)
+                    rhs_scale = vc_plane[j, g][:, n0:n1]
+                nc.tensor.matmul_mx(
+                    out=acc[i, n0][:],
+                    lhsT=c_codes[g][:, rows].bitcast(FP8X4),
+                    lhsT_scale=c_plane[:, g, rows],
+                    rhs=rhs,
+                    rhs_scale=rhs_scale,
+                    start=done == 0,
+                    stop=done == PASSES - 1,
+                )
+                passes_done[i, n0] = done + 1
 
-        def multiply(i, passes, opens, closes):
-            for n, (part, g) in enumerate(passes):
-                mx_pass(i, part, g, opens and n == 0, closes and n == len(passes) - 1)
-
-        def subtract(i):
+        def subtract(i, n0=0, n1=CHUNK):
             j, r = divmod(i, ROW_TILES)
-            if r == 0:
+            if j not in y_sb:
                 y_sb[j] = rotating("y", 5, [P, ROW_TILES, CHUNK], F32)
-            nc.vector.tensor_tensor(out=y_sb[j][:, r, :], in0=x_sb[j][:, r, :], in1=acc[i][:], op=SUB)
+            nc.vector.tensor_tensor(out=y_sb[j][:, r, n0:n1], in0=x_sb[j][:, r, n0:n1], in1=acc[i, n0][:], op=SUB)
 
         def weigh(i):
             j, r = divmod(i, ROW_TILES)
@@ -182,13 +192,14 @@ def tile_mass_weighted_basis_subtraction_k3_kernel(
             y_bf[i] = rotating("y_bf", 8, [P, CHUNK], BF16)
             copy(engine, y_bf[i][:].rearrange("p (u q e) -> p u q e", u=2, e=2), in_word_order(y_sb[j][:, r, :]))
 
-        def weigh_and_round(i):
+        def weigh_and_round(i, n0, n1):
             j, r = divmod(i, ROW_TILES)
-            y_bf[i] = rotating("y_bf", 8, [P, CHUNK], BF16)
+            if n0 == 0:
+                y_bf[i] = rotating("y_bf", 8, [P, CHUNK], BF16)
             nc.vector.tensor_tensor(
-                out=y_bf[i][:].rearrange("p (u q e) -> p u q e", u=2, e=2),
-                in0=in_word_order(y_sb[j][:, r, :]),
-                in1=in_word_order(mass_all[:, cols(j)]),
+                out=y_bf[i][:].rearrange("p (u q e) -> p u q e", u=2, e=2)[:, :, n0 // PACK : n1 // PACK, :],
+                in0=in_word_order(y_sb[j][:, r, n0:n1]),
+                in1=in_word_order(mass_all[:, j * CHUNK + n0 : j * CHUNK + n1]),
                 op=MUL,
             )
 
@@ -235,30 +246,40 @@ def tile_mass_weighted_basis_subtraction_k3_kernel(
                 )
 
         make_identity(nc, ident[:])
-        for plane in (c_plane, va_plane, vb_plane):
+        for plane in (c_plane, va_plane[0], vb_plane[0], va_plane[1], vb_plane[1]):
             nc.vector.memset(plane[:].bitcast(I32), 0)
-        load_scales(nc.gpsimd, va_plane, va_scales, 0)
-        load_scales(nc.gpsimd, vb_plane, vb_scales, VB_ROW)
+        load_scales(nc.gpsimd, va_plane[1], va_scales[:, :, VA_SPLIT[1] :], 0)
+        load_scales(nc.gpsimd, vb_plane[1], vb_scales[:, :, VB_SPLIT[1] :], VB_ROW)
         nc.sync.dma_start(out=mass_run[:], in_=mass.rearrange("(p w) -> p w", w=MASS_RUN))
         load_first_vc(0)
         load_first_vc(1)
         load_c(0)
         load_scales(nc.sync, c_plane, coef_scales, 0)
-        load_c(1)
+        load_scales(nc.sync, va_plane[0], va_scales[:, :, : VA_SPLIT[1]], 0)
         load_va((0, 2))
-        load_vc(SPANS[0], 1)
-        load_vb(SPANS[0])
-        load_vc(SPANS[1], 0)
-        load_x(SPANS[0])
-        load_vc(SPANS[1], 1)
-        load_vb(SPANS[1])
-        load_x(SPANS[1])
-        for span in SPANS[2:]:
-            load_vc(span, 0)
-            load_vc(span, 1)
-            load_va(span)
-            load_vb(span)
-            load_x(span)
+        load_c(1)
+        load_vc((0, 1), 1)
+        load_scales(nc.sync, vb_plane[0], vb_scales[:, :, : VB_SPLIT[1]], VB_ROW)
+        load_vb((0, 1))
+        load_vc((1, 2), 0)
+        load_x((0, 1))
+        load_vc((1, 2), 1)
+        load_vb((1, 2))
+        load_vc((2, 3), 0)
+        load_va((2, 4))
+        load_x((1, 2))
+        load_vc((2, 3), 1)
+        load_vb((2, 3))
+        load_vc((3, 4), 0)
+        load_x((2, 3))
+        load_vc((3, 4), 1)
+        load_vb((3, 4))
+        load_x((3, 4))
+        load_vc((4, 6), 0)
+        load_vc((4, 6), 1)
+        load_va((4, 6))
+        load_vb((4, 6))
+        load_x((4, 6))
 
         mass_words = mass_run[:].bitcast(F32)
         mass_banks = [turn_bank(), turn_bank(), acc_bank([P, 4, P])]
@@ -276,24 +297,29 @@ def tile_mass_weighted_basis_subtraction_k3_kernel(
         interleave("scalar", 0, 1, 352, CHUNK)
         quantize_vc(0, 1)
         for r in range(ROW_TILES):
-            multiply(r, [("c", 0)], True, False)
+            multiply(r, C0)
+        for r in range(ROW_TILES + 2):
+            multiply(r, A)
         for r in range(ROW_TILES):
-            multiply(r, [("a", 0), ("a", 1)], False, False)
-        for r in range(ROW_TILES):
-            multiply(r, [("c", 1)], False, False)
+            multiply(r, C1)
         interleave("vector", 1, 0, 0, CHUNK)
         quantize_vc(1, 0)
         for s in range(TILES):
             j, r = divmod(s, ROW_TILES)
             if j == 0:
-                multiply(s, [("b", 0), ("b", 1)], False, True)
+                multiply(s, B)
             elif j == 1:
                 if r == 0:
-                    for i in range(s, s + ROW_TILES):
-                        multiply(i, [("a", 0), ("a", 1), ("c", 0)], True, False)
-                multiply(s, [("b", 0), ("b", 1), ("c", 1)], False, True)
+                    multiply(s, C0)
+                    multiply(s + 1, C0)
+                    multiply(s + 2, A + C0)
+                    multiply(s + 3, A + C0)
+                multiply(s, B + C1)
+            elif s < TILES - 1:
+                multiply(s, A + B + C0 + C1)
             else:
-                multiply(s, [("a", 0), ("a", 1), ("b", 0), ("b", 1), ("c", 0), ("c", 1)], True, True)
+                for n0 in range(0, CHUNK, P):
+                    multiply(s, A + B + C0 + C1, n0, n0 + P)
             ahead = 1 <= j < CHUNKS - 1
             final = j == CHUNKS - 1
             if r == 0 and j >= 1:
@@ -338,7 +364,7 @@ def tile_mass_weighted_basis_subtraction_k3_kernel(
                 if ahead:
                     round_y("vector", s - 3)
                 if final:
-                    round_y("vector", s - 2)
+                    round_y("scalar", s - 2)
                 weigh(s - 1)
                 if ahead:
                     interleave("scalar", j + 1, 1, HALF, CHUNK)
@@ -374,15 +400,18 @@ def tile_mass_weighted_basis_subtraction_k3_kernel(
         store_y(last - 1, 1)
         round_y("scalar", last - 1)
         turn(last - 3, 2, acc_bank([P, 4, P]))
-        subtract(last)
         unload(last - 3, 2)
-        weigh_and_round(last)
+        subtract(last, 0, P)
+        for n0 in range(P, CHUNK, P):
+            subtract(last, n0, n0 + P)
+            weigh_and_round(last, n0 - P, n0)
+        weigh_and_round(last, CHUNK - P, CHUNK)
         turn(last - 1, 1, acc_bank([P, 4, P]))
         unload(last - 1, 1)
-        quantize_y(last - 3, 2)
         weigh(last)
         store_y(last, 1)
         turn(last, 1, acc_bank([P, 4, P]))
+        quantize_y(last - 3, 2)
         quantize_y(last - 1, 1)
         unload(last, 1)
         store_codes(nc.sync, CHUNKS - 1, CHUNKS, 0, 3 * P)

@@ -79,8 +79,8 @@ def tile_mass_weighted_basis_subtraction_k3_kernel(
             h = 0 if n.start < split[1] else 1
             return planes[h][row:, g, n.start - split[h] : n.stop - split[h]]
 
-        def load_scales(queue, plane, scales, row):
-            for r in range(4):
+        def load_scales(queue, plane, scales, row, rs=range(4)):
+            for r in rs:
                 queue.dma_start(
                     out=plane[row + r : P : 32].bitcast(I32),
                     in_=scales[:, r:16:4, :].rearrange("g q n -> q g n").bitcast(I32),
@@ -248,8 +248,6 @@ def tile_mass_weighted_basis_subtraction_k3_kernel(
         make_identity(nc, ident[:])
         for plane in (c_plane, va_plane[0], vb_plane[0], va_plane[1], vb_plane[1]):
             nc.vector.memset(plane[:].bitcast(I32), 0)
-        load_scales(nc.gpsimd, va_plane[1], va_scales[:, :, VA_SPLIT[1] :], 0)
-        load_scales(nc.gpsimd, vb_plane[1], vb_scales[:, :, VB_SPLIT[1] :], VB_ROW)
         nc.sync.dma_start(out=mass_run[:], in_=mass.rearrange("(p w) -> p w", w=MASS_RUN))
         load_first_vc(0)
         load_first_vc(1)
@@ -259,20 +257,22 @@ def tile_mass_weighted_basis_subtraction_k3_kernel(
         load_va((0, 2))
         load_c(1)
         load_vc((0, 1), 1)
+        load_vc((1, 2), 0)
+        load_vc((1, 2), 1)
         load_scales(nc.sync, vb_plane[0], vb_scales[:, :, : VB_SPLIT[1]], VB_ROW)
         load_vb((0, 1))
-        load_vc((1, 2), 0)
         load_x((0, 1))
-        load_vc((1, 2), 1)
         load_vb((1, 2))
         load_vc((2, 3), 0)
-        load_va((2, 4))
         load_x((1, 2))
         load_vc((2, 3), 1)
         load_vb((2, 3))
+        load_scales(nc.sync, va_plane[1], va_scales[:, :, VA_SPLIT[1] :], 0)
+        load_va((2, 4))
         load_vc((3, 4), 0)
         load_x((2, 3))
         load_vc((3, 4), 1)
+        load_scales(nc.sync, vb_plane[1], vb_scales[:, :, VB_SPLIT[1] :], VB_ROW)
         load_vb((3, 4))
         load_x((3, 4))
         load_vc((4, 6), 0)
@@ -302,97 +302,111 @@ def tile_mass_weighted_basis_subtraction_k3_kernel(
             multiply(r, A)
         for r in range(ROW_TILES):
             multiply(r, C1)
-        interleave("vector", 1, 0, 0, CHUNK)
+        interleave("vector", 1, 0, 0, 352)
+        interleave("scalar", 1, 0, 352, CHUNK)
         quantize_vc(1, 0)
-        for s in range(TILES):
+        interleave("vector", 1, 1, 0, 352)
+        interleave("scalar", 1, 1, 352, CHUNK)
+        quantize_vc(1, 1)
+        multiply(4, C0)
+        multiply(5, C0)
+        multiply(4, C1)
+        multiply(5, C1)
+        for i in range(4):
+            multiply(i, B)
+        subtract(0)
+        subtract(1)
+        subtract(2)
+        weigh(0)
+        subtract(3)
+        weigh(1)
+        weigh(2)
+        weigh(3)
+        multiply(6, A + C0 + C1)
+        multiply(4, B)
+        multiply(5, B)
+        multiply(7, A + C0 + C1)
+        multiply(6, B)
+        multiply(7, B)
+        store_y(0, 4)
+        interleave("scalar", 2, 0, 0, CHUNK)
+        round_y("scalar", 0)
+        round_y("scalar", 1)
+        round_y("scalar", 2)
+        round_y("vector", 3)
+        turn(0, 2, turn_bank())
+        turn(2, 2, turn_bank())
+        subtract(4)
+        subtract(5)
+        quantize_vc(2, 0)
+        interleave("scalar", 2, 1, 0, CHUNK)
+        subtract(6)
+        weigh(4)
+        weigh(5)
+        quantize_vc(2, 1)
+        round_y("scalar", 4)
+
+        for s in range(2 * ROW_TILES, TILES):
             j, r = divmod(s, ROW_TILES)
-            if j == 0:
-                multiply(s, B)
-            elif j == 1:
-                if r == 0:
-                    multiply(s, C0)
-                    multiply(s + 1, C0)
-                    multiply(s + 2, A + C0)
-                    multiply(s + 3, A + C0)
-                multiply(s, B + C1)
-            elif s < TILES - 1:
-                multiply(s, A + B + C0 + C1)
+            final = j == CHUNKS - 1
+            if s < TILES - 1:
+                multiply(s, B + C0 + A + C1)
             else:
                 for n0 in range(0, CHUNK, P):
                     multiply(s, A + B + C0 + C1, n0, n0 + P)
-            ahead = 1 <= j < CHUNKS - 1
-            final = j == CHUNKS - 1
-            if r == 0 and j >= 1:
-                subtract(s - 1)
-                if j > 1:
-                    round_y("vector", s - 2)
-                weigh(s - 1)
+            subtract(s - 1)
+            if not (final and r >= 2):
+                weigh(s - 2)
+            if r == 0:
+                round_y("vector", s - 3)
                 if final:
-                    store_y(s - 2, 2)
                     unload(s - 8, 2)
                     unload(s - 6, 2)
-                    round_y("scalar", s - 1)
+                    round_y("scalar", s - 2)
                 else:
-                    store_y(s - 4, 4)
-                if ahead:
-                    interleave("scalar", j + 1, 0, 0, HALF)
-                    interleave("scalar", j + 1, 0, HALF, CHUNK)
+                    interleave("scalar", j + 1, 0, 0, CHUNK)
             elif r == 1:
-                if j == 0:
-                    interleave("scalar", 1, 1, 0, HALF)
-                    interleave("scalar", 1, 1, HALF, CHUNK)
-                subtract(s - 1)
                 if final:
+                    store_y(s - 3, 2)
+                    round_y("scalar", s - 2)
                     quantize_y(s - 9, ROW_TILES)
+                    weigh(s - 1)
+                    store_y(s - 1, 1)
                     store_codes(nc.sync, j - 3, j - 1, 0, BLOCK)
                     store_scales(0, j - 1, [nc.sync])
-                weigh(s - 1)
-                if ahead:
-                    quantize_vc(j + 1, 0)
-                if final:
-                    store_y(s - 1, 1)
+                    round_y("scalar", s - 1)
                     turn(s - 5, 2, turn_bank())
                     turn(s - 3, 2, turn_bank())
-                if ahead:
+                else:
+                    store_y(s - 5, 4)
+                    quantize_vc(j + 1, 0)
                     interleave("scalar", j + 1, 1, 0, HALF)
-                    if j >= 2:
-                        unload(s - 9, 2)
-                    else:
-                        round_y("scalar", s - 3)
+                    unload(s - 9, 2)
             elif r == 2:
-                subtract(s - 1)
-                if ahead:
-                    round_y("vector", s - 3)
                 if final:
-                    round_y("scalar", s - 2)
-                weigh(s - 1)
-                if ahead:
-                    interleave("scalar", j + 1, 1, HALF, CHUNK)
-                    if j >= 2:
-                        unload(s - 8, 2)
-                if final:
+                    weigh(s - 1)
+                    store_y(s - 1, 1)
                     unload(s - 6, 2)
                     unload(s - 4, 2)
                     round_y("scalar", s - 1)
-                    store_y(s - 1, 1)
-                if j == CHUNKS - 2:
-                    store_y(s - 2, 2)
+                    quantize_y(s - 6, 4)
+                    store_codes(nc.sync, j - 1, j, 0, BLOCK)
+                else:
+                    round_y("vector", s - 4)
+                    interleave("scalar", j + 1, 1, HALF, CHUNK)
+                    unload(s - 8, 2)
             elif r == 3:
                 if final:
-                    quantize_y(s - 7, 4)
-                    store_codes(nc.sync, j - 1, j, 0, BLOCK)
-                subtract(s - 1)
-                if not final:
+                    weigh(s - 1)
+                else:
                     quantize_vc(j + 1, 1)
-                weigh(s - 1)
-                if ahead and j >= 2:
                     quantize_y(s - 11, ROW_TILES)
+                    if j == CHUNKS - 2:
+                        store_y(s - 3, 2)
                     if j % 2 == 1:
                         store_codes(nc.sync, j - 3, j - 1, 0, BLOCK)
-                if not final:
+                    round_y("scalar", s - 4)
                     round_y("scalar", s - 3)
-                    round_y("scalar", s - 2)
-                if ahead:
                     turn(s - 7, 2, turn_bank())
                     turn(s - 5, 2, turn_bank())
 

@@ -33,7 +33,6 @@ ALIGN = 256
 PASSES = 3 * GROUPS
 A, B, C0, C1 = [("a", 0), ("a", 1)], [("b", 0), ("b", 1)], [("c", 0)], [("c", 1)]
 VA_SPLIT = [0, 2 * CHUNK, DOF]
-VB_SPLIT = [0, 3 * CHUNK, DOF]
 
 
 def tile_mass_weighted_basis_subtraction_k3_kernel(
@@ -64,13 +63,14 @@ def tile_mass_weighted_basis_subtraction_k3_kernel(
         c_codes = [kept(f"c_codes{g}", [P, BLOCK], U32) for g in range(GROUPS)]
         c_plane = kept("c_plane", [P, GROUPS, BLOCK], U8)
         va_plane = [kept(f"va_plane{h}", [P, GROUPS, VA_SPLIT[h + 1] - VA_SPLIT[h]], U8) for h in range(2)]
-        vb_plane = [kept(f"vb_plane{h}", [P, GROUPS, VB_SPLIT[h + 1] - VB_SPLIT[h]], U8) for h in range(2)]
-        y_plane = kept("y_plane", [P, CHUNKS, BLOCK], U8)
+        vb_plane = kept("vb_plane", [P, GROUPS, DOF], U8)
+        y_plane = [kept(f"y_plane{h}", [P, BLOCK], U8) for h in range(2)]
         y_codes = kept("y_codes", [P, CHUNKS, BLOCK], U32)
         va_codes, vb_codes, vc_raw, x_sb, first_vc = {}, {}, {}, {}, {}
 
         vc_grouped, vc_codes, vc_plane = {}, {}, {}
-        acc, passes_done, y_sb, y_bf, turned, y_grouped = {}, {}, {}, {}, {}, {}
+        acc, passes_done, y_bf, turned, y_grouped = {}, {}, {}, {}, {}
+        y_sb = {}
 
         def cols(j):
             return slice(j * CHUNK, (j + 1) * CHUNK)
@@ -159,7 +159,7 @@ def tile_mass_weighted_basis_subtraction_k3_kernel(
                     rhs_scale = plane_cols(va_plane, VA_SPLIT, 0, g, n)
                 elif part == "b":
                     rhs = vb_codes[j][:, g, n0:n1].bitcast(FP8X4)
-                    rhs_scale = plane_cols(vb_plane, VB_SPLIT, VB_ROW, g, n)
+                    rhs_scale = vb_plane[VB_ROW:, g, n]
                 else:
                     rhs = vc_codes[j, g][:, n0:n1].bitcast(FP8X4)
                     rhs_scale = vc_plane[j, g][:, n0:n1]
@@ -225,7 +225,7 @@ def tile_mass_weighted_basis_subtraction_k3_kernel(
             m = slice(r * P, (r + count) * P)
             nc.vector.quantize_mx(
                 out=y_codes[:, j, m].bitcast(FP8X4),
-                scales=y_plane[:, j, m],
+                scales=y_plane[j // 4][4 * (j % 4) :, m],
                 in_=y_grouped[j][:, PACK * r * P : PACK * (r + count) * P],
             )
 
@@ -239,15 +239,16 @@ def tile_mass_weighted_basis_subtraction_k3_kernel(
             queue.dma_start(out=dst[:, j0:j1, m0:m1], in_=y_codes[:, j0:j1, m0:m1].bitcast(I32))
 
         def store_scales(j0, j1, queues):
-            for r in range(4):
-                queues[r % len(queues)].dma_start(
-                    out=out_2[j0:j1, r:16:4, :].rearrange("g q m -> q g m").bitcast(I32),
-                    in_=y_plane[r:P:32, j0:j1, :].bitcast(I32),
+            for q in range(QUADS):
+                queues[q % len(queues)].dma_start(
+                    out=out_2[j0:j1, 4 * q : 4 * q + 4, :].bitcast(I32),
+                    in_=y_plane[j0 // 4][32 * q : 32 * q + 4 * (j1 - j0), :].bitcast(I32),
                 )
 
         make_identity(nc, ident[:])
-        for plane in (c_plane, va_plane[0], vb_plane[0], va_plane[1], vb_plane[1]):
+        for plane in (c_plane, va_plane[0], va_plane[1], vb_plane):
             nc.vector.memset(plane[:].bitcast(I32), 0)
+        load_scales(nc.gpsimd, va_plane[1], va_scales[:, :, VA_SPLIT[1] :], 0)
         nc.sync.dma_start(out=mass_run[:], in_=mass.rearrange("(p w) -> p w", w=MASS_RUN))
         load_first_vc(0)
         load_first_vc(1)
@@ -258,21 +259,19 @@ def tile_mass_weighted_basis_subtraction_k3_kernel(
         load_c(1)
         load_vc((0, 1), 1)
         load_vc((1, 2), 0)
-        load_vc((1, 2), 1)
-        load_scales(nc.sync, vb_plane[0], vb_scales[:, :, : VB_SPLIT[1]], VB_ROW)
+        load_scales(nc.sync, vb_plane, vb_scales, VB_ROW)
         load_vb((0, 1))
         load_x((0, 1))
-        load_vb((1, 2))
+        load_vc((1, 2), 1)
         load_vc((2, 3), 0)
-        load_x((1, 2))
+        load_vb((1, 2))
         load_vc((2, 3), 1)
-        load_vb((2, 3))
-        load_scales(nc.sync, va_plane[1], va_scales[:, :, VA_SPLIT[1] :], 0)
+        load_x((1, 2))
         load_va((2, 4))
+        load_vb((2, 3))
         load_vc((3, 4), 0)
-        load_x((2, 3))
         load_vc((3, 4), 1)
-        load_scales(nc.sync, vb_plane[1], vb_scales[:, :, VB_SPLIT[1] :], VB_ROW)
+        load_x((2, 3))
         load_vb((3, 4))
         load_x((3, 4))
         load_vc((4, 6), 0)
@@ -282,13 +281,19 @@ def tile_mass_weighted_basis_subtraction_k3_kernel(
         load_x((4, 6))
 
         mass_words = mass_run[:].bitcast(F32)
+        mass_wide = rotating("y", 5, [P, MASS_WORDS, P], F32)
         mass_banks = [turn_bank(), turn_bank(), acc_bank([P, 4, P])]
-        for w in range(MASS_WORDS):
-            nc.tensor.transpose(mass_banks[w // 4][:, w % 4, :], mass_words[:, w : w + 1].to_broadcast([P, P]), ident[:])
+        for b, bank in enumerate(mass_banks):
+            nc.scalar.copy(
+                out=mass_wide[:, 4 * b : 4 * b + 4, :],
+                in_=mass_words[:, 4 * b : 4 * b + 4].unsqueeze(2).to_broadcast([P, 4, P]),
+            )
+            for w in range(4):
+                nc.tensor.transpose(bank[:, w, :], mass_wide[:, 4 * b + w, :], ident[:])
 
         interleave("vector", 0, 0, 0, HALF)
-        interleave("vector", 0, 0, HALF, 384)
-        interleave("scalar", 0, 0, 384, CHUNK)
+        interleave("vector", 0, 0, HALF, 448)
+        interleave("scalar", 0, 0, 448, CHUNK)
         quantize_vc(0, 0)
         for b, bank in enumerate(mass_banks):
             dst = mass_all[:].bitcast(F32).rearrange("p (n w) -> p n w", w=MASS_WORDS)[:, :, 4 * b : 4 * b + 4]
@@ -305,130 +310,124 @@ def tile_mass_weighted_basis_subtraction_k3_kernel(
         interleave("vector", 1, 0, 0, 352)
         interleave("scalar", 1, 0, 352, CHUNK)
         quantize_vc(1, 0)
-        interleave("vector", 1, 1, 0, 352)
-        interleave("scalar", 1, 1, 352, CHUNK)
-        quantize_vc(1, 1)
-        multiply(4, C0)
-        multiply(5, C0)
-        multiply(4, C1)
-        multiply(5, C1)
+        for i in (4, 5):
+            multiply(i, C0)
         for i in range(4):
             multiply(i, B)
         subtract(0)
         subtract(1)
+        interleave("vector", 1, 1, 0, HALF)
+        interleave("scalar", 1, 1, HALF, CHUNK)
         subtract(2)
-        weigh(0)
+        quantize_vc(1, 1)
         subtract(3)
-        weigh(1)
-        weigh(2)
-        weigh(3)
-        multiply(6, A + C0 + C1)
-        multiply(4, B)
-        multiply(5, B)
-        multiply(7, A + C0 + C1)
-        multiply(6, B)
-        multiply(7, B)
-        store_y(0, 4)
+        for i in (6, 7):
+            multiply(i, A + C0)
+        for i in range(4, 8):
+            multiply(i, C1)
+        for i in range(4, 8):
+            multiply(i, B)
         interleave("scalar", 2, 0, 0, CHUNK)
+        interleave("scalar", 2, 1, 0, CHUNK)
+        for i in range(4):
+            weigh(i)
+        store_y(0, 4)
+        quantize_vc(2, 0)
+        subtract(4)
+        subtract(5)
+        subtract(6)
+        quantize_vc(2, 1)
         round_y("scalar", 0)
         round_y("scalar", 1)
         round_y("scalar", 2)
         round_y("vector", 3)
-        turn(0, 2, turn_bank())
-        turn(2, 2, turn_bank())
-        subtract(4)
-        subtract(5)
-        quantize_vc(2, 0)
-        interleave("scalar", 2, 1, 0, CHUNK)
-        subtract(6)
         weigh(4)
         weigh(5)
-        quantize_vc(2, 1)
-        round_y("scalar", 4)
+        round_y("vector", 4)
 
-        for s in range(2 * ROW_TILES, TILES):
+        for s in range(2 * ROW_TILES, TILES - ROW_TILES):
             j, r = divmod(s, ROW_TILES)
-            final = j == CHUNKS - 1
-            if s < TILES - 1:
-                multiply(s, B + C0 + A + C1)
-            else:
-                for n0 in range(0, CHUNK, P):
-                    multiply(s, A + B + C0 + C1, n0, n0 + P)
+            multiply(s, C0 + A + B + C1)
+            if s == 2 * ROW_TILES:
+                turn(0, 2, turn_bank())
+                turn(2, 2, turn_bank())
             subtract(s - 1)
-            if not (final and r >= 2):
-                weigh(s - 2)
+            weigh(s - 2)
             if r == 0:
                 round_y("vector", s - 3)
-                if final:
-                    unload(s - 8, 2)
-                    unload(s - 6, 2)
-                    round_y("scalar", s - 2)
-                else:
-                    interleave("scalar", j + 1, 0, 0, CHUNK)
+                interleave("scalar", j + 1, 0, 0, CHUNK)
             elif r == 1:
-                if final:
-                    store_y(s - 3, 2)
-                    round_y("scalar", s - 2)
-                    quantize_y(s - 9, ROW_TILES)
-                    weigh(s - 1)
-                    store_y(s - 1, 1)
-                    store_codes(nc.sync, j - 3, j - 1, 0, BLOCK)
-                    store_scales(0, j - 1, [nc.sync])
-                    round_y("scalar", s - 1)
-                    turn(s - 5, 2, turn_bank())
-                    turn(s - 3, 2, turn_bank())
-                else:
-                    store_y(s - 5, 4)
-                    quantize_vc(j + 1, 0)
-                    interleave("scalar", j + 1, 1, 0, HALF)
-                    unload(s - 9, 2)
+                store_y(s - 5, 4)
+                quantize_vc(j + 1, 0)
+                interleave("scalar", j + 1, 1, 0, HALF)
+                unload(s - 9, 2)
             elif r == 2:
-                if final:
-                    weigh(s - 1)
-                    store_y(s - 1, 1)
-                    unload(s - 6, 2)
-                    unload(s - 4, 2)
-                    round_y("scalar", s - 1)
-                    quantize_y(s - 6, 4)
-                    store_codes(nc.sync, j - 1, j, 0, BLOCK)
-                else:
-                    round_y("vector", s - 4)
-                    interleave("scalar", j + 1, 1, HALF, CHUNK)
-                    unload(s - 8, 2)
-            elif r == 3:
-                if final:
-                    weigh(s - 1)
-                else:
-                    quantize_vc(j + 1, 1)
-                    quantize_y(s - 11, ROW_TILES)
-                    if j == CHUNKS - 2:
-                        store_y(s - 3, 2)
-                    if j % 2 == 1:
-                        store_codes(nc.sync, j - 3, j - 1, 0, BLOCK)
-                    round_y("scalar", s - 4)
-                    round_y("scalar", s - 3)
-                    turn(s - 7, 2, turn_bank())
-                    turn(s - 5, 2, turn_bank())
+                interleave("scalar", j + 1, 1, HALF, CHUNK)
+                round_y("scalar", s - 4)
+                unload(s - 8, 2)
+            else:
+                quantize_vc(j + 1, 1)
+                quantize_y(s - 11, ROW_TILES)
+                if j == 3:
+                    store_codes(nc.sync, 0, 2, 0, BLOCK)
+                if j == CHUNKS - 2:
+                    store_y(s - 3, 2)
+                round_y("scalar", s - 4)
+                round_y("scalar", s - 3)
+                turn(s - 7, 2, turn_bank())
+                turn(s - 5, 2, turn_bank())
 
+        multiply(20, C0 + A + B + C1)
+        unload(12, 2)
+        unload(14, 2)
+        subtract(19)
+        weigh(18)
+        weigh(19)
+        store_y(18, 2)
+        round_y("scalar", 17)
+        round_y("scalar", 18)
+        round_y("scalar", 19)
+        quantize_y(12, 4)
+        store_codes(nc.sync, 2, 4, 0, BLOCK)
+        store_scales(0, 4, [nc.sync])
+        multiply(21, C0 + A + B + C1)
+        turn(16, 2, turn_bank())
+        turn(18, 2, turn_bank())
+        subtract(20)
+        subtract(21)
+        weigh(20)
+        weigh(21)
+        store_y(20, 2)
+        unload(16, 2)
+        unload(18, 2)
+        round_y("scalar", 20)
+        round_y("scalar", 21)
+        quantize_y(16, 4)
+        store_codes(nc.sync, 4, 5, 0, BLOCK)
+        multiply(22, C0 + A + B + C1)
         last = TILES - 1
-        store_y(last - 1, 1)
-        round_y("scalar", last - 1)
-        turn(last - 3, 2, acc_bank([P, 4, P]))
-        unload(last - 3, 2)
+        for n0 in range(0, CHUNK, P):
+            multiply(last, C0 + A + B + C1, n0, n0 + P)
+        subtract(22)
         subtract(last, 0, P)
+        weigh(22)
+        store_y(22, 1)
+        round_y("scalar", 22)
+        turn(20, 2, acc_bank([P, 4, P]))
+        unload(20, 2)
         for n0 in range(P, CHUNK, P):
             subtract(last, n0, n0 + P)
             weigh_and_round(last, n0 - P, n0)
         weigh_and_round(last, CHUNK - P, CHUNK)
-        turn(last - 1, 1, acc_bank([P, 4, P]))
-        unload(last - 1, 1)
+        turn(22, 1, acc_bank([P, 4, P]))
+        unload(22, 1)
         weigh(last)
         store_y(last, 1)
+        quantize_y(20, 2)
         turn(last, 1, acc_bank([P, 4, P]))
-        quantize_y(last - 3, 2)
-        quantize_y(last - 1, 1)
+        quantize_y(22, 1)
         unload(last, 1)
-        store_codes(nc.sync, CHUNKS - 1, CHUNKS, 0, 3 * P)
+        store_codes(nc.scalar, CHUNKS - 1, CHUNKS, 0, 3 * P)
         quantize_y(last, 1)
-        store_codes(nc.scalar, CHUNKS - 1, CHUNKS, 3 * P, BLOCK)
         store_scales(CHUNKS - 2, CHUNKS, [nc.sync, nc.scalar])
+        store_codes(nc.sync, CHUNKS - 1, CHUNKS, 3 * P, BLOCK)

from contextlib import ExitStack

import concourse.mybir as mybir
from concourse.masks import make_identity

BLOCK, MODES, DOF = 512, 1024, 3072
FLOPS = 3 * 2 * BLOCK * MODES * DOF

F32 = mybir.dt.float32
BF16 = mybir.dt.bfloat16
I32 = mybir.dt.int32
U32 = mybir.dt.uint32
U8 = mybir.dt.uint8
FP8X4 = mybir.dt.float8_e4m3fn_x4
FP4X4 = mybir.dt.float4_e2m1fn_x4
SUB = mybir.AluOpType.subtract
MUL = mybir.AluOpType.mult

P = 128
PACK = 4
K_PASS = P * PACK
GROUPS = MODES // K_PASS
CHUNK = 512
CHUNKS = DOF // CHUNK
ROW_TILES = BLOCK // P
TILES = CHUNKS * ROW_TILES
HALF = CHUNK // 2
QUADS = 4
VB_ROW = 4
MASS_RUN = DOF // P
MASS_WORDS = MASS_RUN // 2
ALIGN = 256
PASSES = 3 * GROUPS
A, B, C0, C1 = [("a", 0), ("a", 1)], [("b", 0), ("b", 1)], [("c", 0)], [("c", 1)]
VA_SPLIT = [0, 2 * CHUNK, DOF]


def tile_mass_weighted_basis_subtraction_k3_kernel(
    tc, coef_words, coef_scales, va_words, va_scales, vb_words, vb_scales, vc, x, mass, out_0, out_1, out_2
):
    nc = tc.nc
    with ExitStack() as ctx:
        keep = ctx.enter_context(tc.tile_pool(name="keep", bufs=1))
        work = ctx.enter_context(tc.tile_pool(name="work", bufs=1))
        psum = ctx.enter_context(tc.psum_pool(name="psum", bufs=1))
        ctx.enter_context(tc.manual_schedule())

        def kept(name, shape, dtype):
            return keep.tile(shape, dtype, name=name, align_bytes=ALIGN)

        def rotating(tag, bufs, shape, dtype):
            return work.tile(shape, dtype, name=tag, tag=tag, bufs=bufs, align_bytes=ALIGN)

        def acc_bank(shape):
            return psum.tile(shape, F32, name="acc", tag="acc", bufs=6)

        def turn_bank():
            return psum.tile([P, 4, P], F32, name="turn", tag="turn", bufs=2)

        ident = kept("ident", [P, P], F32)
        mass_run = kept("mass_run", [P, MASS_RUN], BF16)
        mass_all = kept("mass_all", [P, DOF], BF16)
        c_codes = [kept(f"c_codes{g}", [P, BLOCK], U32) for g in range(GROUPS)]
        c_plane = kept("c_plane", [P, GROUPS, BLOCK], U8)
        va_plane = [kept(f"va_plane{h}", [P, GROUPS, VA_SPLIT[h + 1] - VA_SPLIT[h]], U8) for h in range(2)]
        vb_plane = kept("vb_plane", [P, GROUPS, DOF], U8)
        y_plane = [kept(f"y_plane{h}", [P, BLOCK], U8) for h in range(2)]
        y_codes = kept("y_codes", [P, CHUNKS, BLOCK], U32)
        va_codes, vb_codes, vc_raw, x_sb, first_vc = {}, {}, {}, {}, {}

        vc_grouped, vc_codes, vc_plane = {}, {}, {}
        acc, passes_done, y_bf, turned, y_grouped = {}, {}, {}, {}, {}
        y_sb = {}

        def cols(j):
            return slice(j * CHUNK, (j + 1) * CHUNK)

        def plane_cols(planes, split, row, g, n):
            h = 0 if n.start < split[1] else 1
            return planes[h][row:, g, n.start - split[h] : n.stop - split[h]]

        def load_scales(queue, plane, scales, row, rs=range(4)):
            for r in rs:
                queue.dma_start(
                    out=plane[row + r : P : 32].bitcast(I32),
                    in_=scales[:, r:16:4, :].rearrange("g q n -> q g n").bitcast(I32),
                )

        def load_c(g):
            nc.sync.dma_start(
                out=c_codes[g][:].bitcast(I32), in_=coef_words[g].rearrange("p n t -> p (n t)").bitcast(I32)
            )

        def span_tile(name, span, lead, per_column, dtype, by_chunk):
            first, end = span
            tile = kept(f"{name}{first}", [P, lead, (end - first) * CHUNK * per_column], dtype)
            for j in range(first, end):
                by_chunk[j] = tile[:, :, (j - first) * CHUNK * per_column : (j - first + 1) * CHUNK * per_column]
            return tile, slice(first * CHUNK, end * CHUNK)

        def load_vc(span, g):
            tile, n = span_tile(f"vc_raw{g}_", span, PACK, 1, BF16, vc_raw.setdefault(g, {}))
            rows = vc[g * K_PASS : (g + 1) * K_PASS, n]
            nc.sync.dma_start(out=tile[:], in_=rows.rearrange("(p t) n -> p t n", t=PACK))

        def load_first_vc(h):
            first_vc[h] = kept(f"first_vc{h}", [P, PACK, HALF], BF16)
            rows = vc[:K_PASS, h * HALF : (h + 1) * HALF]
            nc.sync.dma_start(out=first_vc[h][:], in_=rows.rearrange("(p t) n -> p t n", t=PACK))

        def load_va(span):
            tile, n = span_tile("va_codes", span, GROUPS, 2, U8, va_codes)
            src = va_words.rearrange("g p b -> p g b")[:, :, 2 * n.start : 2 * n.stop]
            nc.sync.dma_start(out=tile[:].bitcast(I32), in_=src.bitcast(I32))

        def load_vb(span):
            tile, n = span_tile("vb_codes", span, GROUPS, 1, U32, vb_codes)
            src = vb_words.rearrange("g p n t -> p g (n t)")[:, :, 4 * n.start : 4 * n.stop]
            nc.sync.dma_start(out=tile[:].bitcast(I32), in_=src.bitcast(I32))

        def load_x(span):
            tile, n = span_tile("x", span, ROW_TILES, 1, BF16, x_sb)
            nc.sync.dma_start(out=tile[:], in_=x.rearrange("(r p) n -> p r n", p=P)[:, :, n])

        def interleave(engine, j, g, n0, n1):
            if n0 == 0:
                vc_grouped[j, g] = rotating("vc_grouped", 3, [P, CHUNK * PACK], BF16)
            dst = vc_grouped[j, g][:, n0 * PACK : n1 * PACK]
            if (j, g) == (0, 0):
                h = n0 // HALF
                src = first_vc[h][:, :, n0 - h * HALF : n1 - h * HALF]
            else:
                src = vc_raw[g][j][:, :, n0:n1]
            copy(engine, dst.rearrange("p (c i t) -> p c t i", i=4, t=PACK), src.rearrange("p t (c i) -> p c t i", i=4))

        def copy(engine, out, in_):
            if engine == "vector":
                nc.vector.tensor_copy(out=out, in_=in_)
            else:
                nc.scalar.copy(out=out, in_=in_)

        def quantize_vc(j, g):
            vc_codes[j, g] = rotating("vc_codes", 4, [P, CHUNK], U32)
            vc_plane[j, g] = rotating("vc_plane", 4, [P, CHUNK], U8)
            nc.vector.quantize_mx(
                out=vc_codes[j, g][:].bitcast(FP8X4), scales=vc_plane[j, g][:], in_=vc_grouped[j, g][:]
            )

        def multiply(i, passes, n0=0, n1=CHUNK):
            j, r = divmod(i, ROW_TILES)
            rows = slice(r * P, (r + 1) * P)
            n = slice(j * CHUNK + n0, j * CHUNK + n1)
            for part, g in passes:
                done = passes_done.get((i, n0), 0)
                if done == 0:
                    acc[i, n0] = acc_bank([P, n1 - n0])
                if part == "a":
                    rhs = va_codes[j][:, g, 2 * n0 : 2 * n1].bitcast(FP4X4)
                    rhs_scale = plane_cols(va_plane, VA_SPLIT, 0, g, n)
                elif part == "b":
                    rhs = vb_codes[j][:, g, n0:n1].bitcast(FP8X4)
                    rhs_scale = vb_plane[VB_ROW:, g, n]
                else:
                    rhs = vc_codes[j, g][:, n0:n1].bitcast(FP8X4)
                    rhs_scale = vc_plane[j, g][:, n0:n1]
                nc.tensor.matmul_mx(
                    out=acc[i, n0][:],
                    lhsT=c_codes[g][:, rows].bitcast(FP8X4),
                    lhsT_scale=c_plane[:, g, rows],
                    rhs=rhs,
                    rhs_scale=rhs_scale,
                    start=done == 0,
                    stop=done == PASSES - 1,
                )
                passes_done[i, n0] = done + 1

        def subtract(i, n0=0, n1=CHUNK):
            j, r = divmod(i, ROW_TILES)
            if j not in y_sb:
                y_sb[j] = rotating("y", 5, [P, ROW_TILES, CHUNK], F32)
            nc.vector.tensor_tensor(out=y_sb[j][:, r, n0:n1], in0=x_sb[j][:, r, n0:n1], in1=acc[i, n0][:], op=SUB)

        def weigh(i):
            j, r = divmod(i, ROW_TILES)
            nc.vector.tensor_tensor(out=y_sb[j][:, r, :], in0=y_sb[j][:, r, :], in1=mass_all[:, cols(j)], op=MUL)

        def in_word_order(ap):
            return ap.rearrange("p (q u e) -> p u q e", u=2, e=2)

        def round_y(engine, i):
            j, r = divmod(i, ROW_TILES)
            y_bf[i] = rotating("y_bf", 8, [P, CHUNK], BF16)
            copy(engine, y_bf[i][:].rearrange("p (u q e) -> p u q e", u=2, e=2), in_word_order(y_sb[j][:, r, :]))

        def weigh_and_round(i, n0, n1):
            j, r = divmod(i, ROW_TILES)
            if n0 == 0:
                y_bf[i] = rotating("y_bf", 8, [P, CHUNK], BF16)
            nc.vector.tensor_tensor(
                out=y_bf[i][:].rearrange("p (u q e) -> p u q e", u=2, e=2)[:, :, n0 // PACK : n1 // PACK, :],
                in0=in_word_order(y_sb[j][:, r, n0:n1]),
                in1=in_word_order(mass_all[:, j * CHUNK + n0 : j * CHUNK + n1]),
                op=MUL,
            )

        def turn(first, count, bank):
            turned[first] = bank
            for n in range(count):
                words = y_bf[first + n][:].bitcast(F32)
                for u in range(2):
                    nc.tensor.transpose(turned[first][:, 2 * n + u, :], words[:, u * P : (u + 1) * P], ident[:])

        def unload(first, count):
            j, r = divmod(first, ROW_TILES)
            if r == 0:
                y_grouped[j] = rotating("y_grouped", 2, [P, BLOCK * PACK], BF16)
            dst = y_grouped[j][:].bitcast(F32)[:, 2 * r * P : 2 * (r + count) * P]
            nc.scalar.copy(
                out=dst.rearrange("p (n m u) -> p n m u", n=count, u=2),
                in_=turned[first][:, : 2 * count, :].rearrange("p (n u) m -> p n m u", u=2),
            )

        def quantize_y(first, count):
            j, r = divmod(first, ROW_TILES)
            m = slice(r * P, (r + count) * P)
            nc.vector.quantize_mx(
                out=y_codes[:, j, m].bitcast(FP8X4),
                scales=y_plane[j // 4][4 * (j % 4) :, m],
                in_=y_grouped[j][:, PACK * r * P : PACK * (r + count) * P],
            )

        def store_y(first, count):
            j, r = divmod(first, ROW_TILES)
            dst = out_0.rearrange("(r p) n -> p r n", p=P)[:, r : r + count, cols(j)]
            nc.sync.dma_start(out=dst, in_=y_sb[j][:, r : r + count, :])

        def store_codes(queue, j0, j1, m0, m1):
            dst = out_1.rearrange("g p m t -> p g (m t)").bitcast(I32)
            queue.dma_start(out=dst[:, j0:j1, m0:m1], in_=y_codes[:, j0:j1, m0:m1].bitcast(I32))

        def store_scales(j0, j1, queues):
            for q in range(QUADS):
                queues[q % len(queues)].dma_start(
                    out=out_2[j0:j1, 4 * q : 4 * q + 4, :].bitcast(I32),
                    in_=y_plane[j0 // 4][32 * q : 32 * q + 4 * (j1 - j0), :].bitcast(I32),
                )

        make_identity(nc, ident[:])
        for plane in (c_plane, va_plane[0], va_plane[1], vb_plane):
            nc.vector.memset(plane[:].bitcast(I32), 0)
        load_scales(nc.gpsimd, va_plane[1], va_scales[:, :, VA_SPLIT[1] :], 0)
        nc.sync.dma_start(out=mass_run[:], in_=mass.rearrange("(p w) -> p w", w=MASS_RUN))
        load_first_vc(0)
        load_first_vc(1)
        load_c(0)
        load_scales(nc.sync, c_plane, coef_scales, 0)
        load_scales(nc.sync, va_plane[0], va_scales[:, :, : VA_SPLIT[1]], 0)
        load_va((0, 2))
        load_c(1)
        load_vc((0, 1), 1)
        load_vc((1, 2), 0)
        load_scales(nc.sync, vb_plane, vb_scales, VB_ROW)
        load_vb((0, 1))
        load_x((0, 1))
        load_vc((1, 2), 1)
        load_vc((2, 3), 0)
        load_vb((1, 2))
        load_vc((2, 3), 1)
        load_x((1, 2))
        load_va((2, 4))
        load_vb((2, 3))
        load_vc((3, 4), 0)
        load_vc((3, 4), 1)
        load_x((2, 3))
        load_vb((3, 4))
        load_x((3, 4))
        load_vc((4, 6), 0)
        load_vc((4, 6), 1)
        load_va((4, 6))
        load_vb((4, 6))
        load_x((4, 6))

        mass_words = mass_run[:].bitcast(F32)
        mass_wide = rotating("y", 5, [P, MASS_WORDS, P], F32)
        mass_banks = [turn_bank(), turn_bank(), acc_bank([P, 4, P])]
        for b, bank in enumerate(mass_banks):
            nc.scalar.copy(
                out=mass_wide[:, 4 * b : 4 * b + 4, :],
                in_=mass_words[:, 4 * b : 4 * b + 4].unsqueeze(2).to_broadcast([P, 4, P]),
            )
            for w in range(4):
                nc.tensor.transpose(bank[:, w, :], mass_wide[:, 4 * b + w, :], ident[:])

        interleave("vector", 0, 0, 0, HALF)
        interleave("vector", 0, 0, HALF, 448)
        interleave("scalar", 0, 0, 448, CHUNK)
        quantize_vc(0, 0)
        for b, bank in enumerate(mass_banks):
            dst = mass_all[:].bitcast(F32).rearrange("p (n w) -> p n w", w=MASS_WORDS)[:, :, 4 * b : 4 * b + 4]
            nc.scalar.copy(out=dst, in_=bank[:].rearrange("p w n -> p n w"))
        interleave("vector", 0, 1, 0, 352)
        interleave("scalar", 0, 1, 352, CHUNK)
        quantize_vc(0, 1)
        for r in range(ROW_TILES):
            multiply(r, C0)
        for r in range(ROW_TILES + 2):
            multiply(r, A)
        for r in range(ROW_TILES):
            multiply(r, C1)
        interleave("vector", 1, 0, 0, 352)
        interleave("scalar", 1, 0, 352, CHUNK)
        quantize_vc(1, 0)
        for i in (4, 5):
            multiply(i, C0)
        for i in range(4):
            multiply(i, B)
        subtract(0)
        subtract(1)
        interleave("vector", 1, 1, 0, HALF)
        interleave("scalar", 1, 1, HALF, CHUNK)
        subtract(2)
        quantize_vc(1, 1)
        subtract(3)
        for i in (6, 7):
            multiply(i, A + C0)
        for i in range(4, 8):
            multiply(i, C1)
        for i in range(4, 8):
            multiply(i, B)
        interleave("scalar", 2, 0, 0, CHUNK)
        interleave("scalar", 2, 1, 0, CHUNK)
        for i in range(4):
            weigh(i)
        store_y(0, 4)
        quantize_vc(2, 0)
        subtract(4)
        subtract(5)
        subtract(6)
        quantize_vc(2, 1)
        round_y("scalar", 0)
        round_y("scalar", 1)
        round_y("scalar", 2)
        round_y("vector", 3)
        weigh(4)
        weigh(5)
        round_y("vector", 4)

        for s in range(2 * ROW_TILES, TILES - ROW_TILES):
            j, r = divmod(s, ROW_TILES)
            multiply(s, C0 + A + B + C1)
            if s == 2 * ROW_TILES:
                turn(0, 2, turn_bank())
                turn(2, 2, turn_bank())
            subtract(s - 1)
            weigh(s - 2)
            if r == 0:
                round_y("vector", s - 3)
                interleave("scalar", j + 1, 0, 0, CHUNK)
            elif r == 1:
                store_y(s - 5, 4)
                quantize_vc(j + 1, 0)
                interleave("scalar", j + 1, 1, 0, HALF)
                unload(s - 9, 2)
            elif r == 2:
                interleave("scalar", j + 1, 1, HALF, CHUNK)
                round_y("scalar", s - 4)
                unload(s - 8, 2)
            else:
                quantize_vc(j + 1, 1)
                quantize_y(s - 11, ROW_TILES)
                if j == 3:
                    store_codes(nc.sync, 0, 2, 0, BLOCK)
                if j == CHUNKS - 2:
                    store_y(s - 3, 2)
                round_y("scalar", s - 4)
                round_y("scalar", s - 3)
                turn(s - 7, 2, turn_bank())
                turn(s - 5, 2, turn_bank())

        multiply(20, C0 + A + B + C1)
        unload(12, 2)
        unload(14, 2)
        subtract(19)
        weigh(18)
        weigh(19)
        store_y(18, 2)
        round_y("scalar", 17)
        round_y("scalar", 18)
        round_y("scalar", 19)
        quantize_y(12, 4)
        store_codes(nc.sync, 2, 4, 0, BLOCK)
        store_scales(0, 4, [nc.sync])
        multiply(21, C0 + A + B + C1)
        turn(16, 2, turn_bank())
        turn(18, 2, turn_bank())
        subtract(20)
        subtract(21)
        weigh(20)
        weigh(21)
        store_y(20, 2)
        unload(16, 2)
        unload(18, 2)
        round_y("scalar", 20)
        round_y("scalar", 21)
        quantize_y(16, 4)
        store_codes(nc.sync, 4, 5, 0, BLOCK)
        multiply(22, C0 + A + B + C1)
        last = TILES - 1
        for n0 in range(0, CHUNK, P):
            multiply(last, C0 + A + B + C1, n0, n0 + P)
        subtract(22)
        subtract(last, 0, P)
        weigh(22)
        store_y(22, 1)
        round_y("scalar", 22)
        turn(20, 2, acc_bank([P, 4, P]))
        unload(20, 2)
        for n0 in range(P, CHUNK, P):
            subtract(last, n0, n0 + P)
            weigh_and_round(last, n0 - P, n0)
        weigh_and_round(last, CHUNK - P, CHUNK)
        turn(22, 1, acc_bank([P, 4, P]))
        unload(22, 1)
        weigh(last)
        store_y(last, 1)
        quantize_y(20, 2)
        turn(last, 1, acc_bank([P, 4, P]))
        quantize_y(22, 1)
        unload(last, 1)
        store_codes(nc.scalar, CHUNKS - 1, CHUNKS, 0, 3 * P)
        quantize_y(last, 1)
        store_scales(CHUNKS - 2, CHUNKS, [nc.sync, nc.scalar])
        store_codes(nc.sync, CHUNKS - 1, CHUNKS, 3 * P, BLOCK)
